import numpy as np
import ml_dtypes


def mxq(x, axis, fmt="e4m3"):
    dtype, down = {"e4m3": (ml_dtypes.float8_e4m3fn, 7), "e5m2": (ml_dtypes.float8_e5m2, 14)}[fmt]
    v = np.moveaxis(np.asarray(x, np.float32).astype(ml_dtypes.bfloat16).astype(np.float64), axis, -1)
    blocks = v.reshape(v.shape[:-1] + (-1, 32))
    amax = np.abs(blocks).max(-1, keepdims=True)
    byte = np.maximum(np.where(amax > 0, np.frexp(amax)[1] - 1 + 127, 0) - down, 1)
    scale = np.exp2(byte - 127.0)
    codes = (blocks / scale).astype(np.float32).astype(dtype).astype(np.float64)
    return np.moveaxis((codes * scale).reshape(v.shape), -1, axis)


WIDE = False


def mx_kscale(k):
    if not WIDE:
        return np.ones(k)
    levels = np.array([10, -10, 5, -5, 0])
    if k % 512:
        return np.exp2(np.random.permutation(np.resize(levels, k // 32))).repeat(32)
    a = np.empty((k // 512, 16))
    for p in range(k // 512):
        a[p, :8] = np.random.permutation(np.resize(levels, 8))
        for g in range(8):
            far = levels[np.abs(levels - a[p, g]) >= 10]
            a[p, g + 8] = far[np.random.randint(len(far))]
    return np.exp2(a.ravel()).repeat(32)


def f64(x):
    return np.asarray(x).astype(np.float64)


def striped(idx):
    return np.tile(idx.reshape(-1, 16).T, (8, 1)).astype(np.uint16)


def unstriped(offs):
    return offs[:16].T.reshape(-1).astype(np.int64)


def relu(v):
    return np.maximum(v, 0.0)

def planes(y):
    n, m = y.shape
    v = y.astype(np.float32).astype(ml_dtypes.bfloat16).astype(np.float64).reshape(n // 32, 32, m)
    top = np.abs(v).max(1)
    byte = np.clip(np.where(top > 0, np.frexp(top)[1] - 1 + 127 - 7, 1), 1, 254)
    codes = (v * np.exp2(127.0 - byte)[:, None, :]).reshape(n, m).astype(np.float32).astype(ml_dtypes.float8_e4m3fn).view(np.uint8)
    words = codes.reshape(n // 512, 128, 4, m).transpose(0, 1, 3, 2)
    return np.ascontiguousarray(words), np.ascontiguousarray(byte.astype(np.uint8).reshape(n // 512, 16, m))


K, T, S, V, H = 512, 1024, 512, 256, 512


def setup_inputs():
    n = np.random.standard_normal
    s = mx_kscale(K)[:, None]
    u = mx_kscale(H)
    return {
        "xT": (n((K, T)) * s).astype(np.float32),
        "w1": (n((K, H)) / np.sqrt(2 * K) / s * u).astype(np.float32),
        "w2": (n((K, H)) / np.sqrt(2 * K) / s * u).astype(np.float32),
        "w3": (n((H, H)) / np.sqrt(H) / u[:, None]).astype(np.float32),
        "offs": striped(np.random.permutation(T)[:S]),
        "cen": striped(np.random.permutation(S)[:V]),
        "pos1": striped(np.random.permutation(S)[:V]),
        "pos2": striped(np.random.permutation(S)[:V]),
        "pos3": striped(np.random.permutation(S)[:V]),
        "pos4": striped(np.random.permutation(S)[:V]),
    }


def reference(xT, w1, w2, w3, offs, cen, pos1, pos2, pos3, pos4):
    xq = mxq(f64(xT)[:, unstriped(offs)], 0, "e4m3")
    y = mxq(f64(w1), 0, "e4m3").T @ xq
    yc = y[:, unstriped(cen)]
    e = mxq(f64(w2), 0, "e4m3").T @ xq
    z = np.maximum(np.maximum(np.maximum(relu(yc + e[:, unstriped(pos1)]), relu(yc + e[:, unstriped(pos2)])), relu(yc + e[:, unstriped(pos3)])), relu(yc + e[:, unstriped(pos4)]))
    out_0 = mxq(f64(w3), 0, "e4m3").T @ mxq(z, 0, "e4m3")
    return (out_0,) + planes(out_0)

@@ -1,0 +1,225 @@
+from contextlib import ExitStack
+
+import concourse.mybir as mybir
+
+K, T, S, V, H = 512, 1024, 512, 256, 512
+FLOPS = 2 * (2 * K * H * S + H * H * V)
+
+F32 = mybir.dt.float32
+BF16 = mybir.dt.bfloat16
+I32 = mybir.dt.int32
+U32 = mybir.dt.uint32
+U16 = mybir.dt.uint16
+U8 = mybir.dt.uint8
+FP8X4 = mybir.dt.float8_e4m3fn_x4
+ADD = mybir.AluOpType.add
+MAX = mybir.AluOpType.max
+RELU = mybir.ActivationFunctionType.Relu
+
+P = 128
+PACK = 4
+LIST_ROWS = 16
+HALF_S = S // 2
+HALF_V = V // 2
+
+
+def tile_picked_edgecv_relu_lo_kernel(
+    tc, xT, w1, w2, w3, offs, cen, pos1, pos2, pos3, pos4, out_0, out_1, out_2
+):
+    nc = tc.nc
+    with ExitStack() as ctx:
+        keep = ctx.enter_context(tc.tile_pool(name="keep", bufs=1))
+        psum = ctx.enter_context(tc.psum_pool(name="psum", bufs=1))
+
+        def sb(name, shape, dtype):
+            return keep.tile(shape, dtype, name=name, align_bytes=64)
+
+        def load_list(name, src):
+            tile = keep.tile([P, src.shape[1]], U16, name=name)
+            nc.sync.dma_start(tile[:], src)
+            return tile
+
+        def entries(lst, lo, n):
+            return lst[:, lo // LIST_ROWS : (lo + n) // LIST_ROWS]
+
+        def quantize(codes, scales, grouped):
+            nc.vector.quantize_mx(out=codes.bitcast(FP8X4), scales=scales, in_=grouped.rearrange("p c j -> p (c j)"))
+
+        def product(acc, w_codes, w_scales, x_codes, x_scales):
+            nc.tensor.matmul_mx(
+                out=acc, lhsT=w_codes.bitcast(FP8X4), lhsT_scale=w_scales,
+                rhs=x_codes.bitcast(FP8X4), rhs_scale=x_scales, start=True, stop=True,
+            )
+
+        def weave_views(grouped, planes):
+            return (
+                grouped.rearrange("p (c i) j -> p c j i", i=4),
+                planes.rearrange("p j (c i) -> p c j i", i=4),
+            )
+
+        offs_t = load_list("offs_t", offs)
+        x_rows = xT.rearrange("(p j) c -> j p c", j=PACK)
+        x_plane = [sb(f"x_plane{j}", [P, T], F32) for j in range(PACK)]
+        for j in range(PACK):
+            nc.sync.dma_start(x_plane[j][:], x_rows[j])
+        w2_raw = sb("w2_raw", [P, PACK, H], F32)
+        nc.sync.dma_start(w2_raw[:], w2.rearrange("(p j) c -> p j c", j=PACK))
+        pos_t = [load_list(f"pos{d}_t", src) for d, src in enumerate((pos1, pos2, pos3, pos4))]
+        w1_raw = sb("w1_raw", [P, PACK, H], F32)
+        nc.sync.dma_start(w1_raw[:], w1.rearrange("(p j) c -> p j c", j=PACK))
+        cen_t = load_list("cen_t", cen)
+        w3_raw = sb("w3_raw", [P, PACK, H], F32)
+        w3_rows = w3.rearrange("(b t q) c -> q b t c", t=PACK, q=8)
+        for q in (0, 4, 1, 5, 2, 6, 3, 7):
+            nc.sync.dma_start(w3_raw[q:P:8, :, :], w3_rows[q])
+
+        picked = [sb(f"picked{h}", [P, PACK, HALF_S], F32) for h in range(2)]
+        for j in range(PACK):
+            for h in range(2):
+                nc.vector.tensor_copy(picked[h][:, j, :], x_plane[j][:].indirect(entries(offs_t, h * HALF_S, HALF_S)))
+        x_grouped = [sb(f"x_grouped{h}", [P, HALF_S, PACK], BF16) for h in range(2)]
+        dst, src = weave_views(x_grouped[0][:], picked[0][:])
+        nc.scalar.copy(dst, src)
+        dst, src = weave_views(x_grouped[1][:], picked[1][:])
+        nc.vector.tensor_copy(dst, src)
+        x_codes = sb("x_codes", [P, S], U32)
+        x_scales = sb("x_scales", [P, S], U8)
+        for h in range(2):
+            cols = slice(h * HALF_S, (h + 1) * HALF_S)
+            quantize(x_codes[:, cols], x_scales[:, cols], x_grouped[h][:])
+
+        def hidden_weights(name, w_raw, t):
+            grouped = sb(f"{name}_grouped{t}", [P, P, PACK], BF16)
+            nc.scalar.copy(
+                grouped[:].rearrange("p (b u i) j -> p b u j i", u=2, i=4),
+                w_raw[:].rearrange("p j (b t u i) -> p t b u j i", t=PACK, u=2, i=4)[:, t],
+            )
+            codes = sb(f"{name}_codes{t}", [P, P], U32)
+            scales = sb(f"{name}_scales{t}", [P, P], U8)
+            quantize(codes[:], scales[:], grouped[:])
+            return codes, scales
+
+        def hidden_rows(name, w_raw, t, bank):
+            codes, scales = hidden_weights(name, w_raw, t)
+            acc = psum.tile([P, S], F32, name=f"{name}_acc{t}", tag=f"bank{bank}")
+            product(acc[:], codes[:], scales[:], x_codes[:], x_scales[:])
+            rows = sb(f"{name}_rows{t}", [P, S], F32)
+            nc.scalar.copy(rows[:], acc[:])
+            return rows
+
+        codes, scales = hidden_weights("e", w2_raw, 0)
+        e_first = sb("e_rows0", [P, S], F32)
+        for h in range(2):
+            cols = slice(h * HALF_S, (h + 1) * HALF_S)
+            acc = psum.tile([P, HALF_S], F32, name=f"e_first_acc{h}", tag=f"bank{h}")
+            product(acc[:], codes[:], scales[:], x_codes[:, cols], x_scales[:, cols])
+            if h == 0:
+                nc.scalar.copy(e_first[:, cols], acc[:])
+            else:
+                nc.vector.tensor_copy(e_first[:, cols], acc[:])
+        e_rows = [e_first]
+        y_rows = []
+
+        sums = [sb(f"sums{h}", [P, PACK, HALF_V], F32) for h in range(2)]
+        steps = [(0, 0, V), (1, 0, V), (2, 0, V), (3, 0, HALF_V), (3, HALF_V, HALF_V)]
+
+        w3_grouped = sb("w3_grouped", [P, H, PACK], BF16)
+        w3_codes = sb("w3_codes", [P, H], U32)
+        w3_scales = sb("w3_scales", [P, H], U8)
+
+        def w3_deal(part):
+            ms = slice(32 * part, 32 * (part + 1))
+            nc.scalar.copy(
+                w3_grouped[:].rearrange("p (t m) j -> p m j t", t=PACK)[:, ms],
+                w3_raw[:].rearrange("p j (m t) -> p m j t", t=PACK)[:, ms],
+            )
+
+        out_codes = sb("out_codes", [P, V], U32)
+        out_scales = sb("out_scales", [P, V], U8)
+        out_rows = out_0.rearrange("(p t) v -> p t v", t=PACK)
+        words_out = out_1.rearrange("z p c r -> p (z c r)").bitcast(I32)
+
+        def finish(h):
+            cols = slice(h * HALF_V, (h + 1) * HALF_V)
+            z_grouped = sb(f"z_grouped{h}", [P, HALF_V, PACK], BF16)
+            dst, src = weave_views(z_grouped[:], sums[h][:])
+            if h == 0:
+                nc.scalar.activation(dst, src, RELU)
+            else:
+                nc.vector.tensor_scalar_max(dst, src, 0.0)
+            z_codes = sb(f"z_codes{h}", [P, HALF_V], U32)
+            z_scales = sb(f"z_scales{h}", [P, HALF_V], U8)
+            quantize(z_codes[:], z_scales[:], z_grouped[:])
+            acc = psum.tile([P, PACK, HALF_V], F32, name=f"out_acc{h}", tag=f"bank{6 + h}")
+            for t in range(PACK):
+                ms = slice(t * P, (t + 1) * P)
+                product(acc[:, t, :], w3_codes[:, ms], w3_scales[:, ms], z_codes[:], z_scales[:])
+            out_grouped = sb(f"out_grouped{h}", [P, HALF_V, PACK], BF16)
+            result = sb(f"result{h}", [P, PACK, HALF_V], F32)
+            if h == 0:
+                nc.scalar.copy(result[:], acc[:])
+                nc.scalar.copy(out_grouped[:], acc[:].rearrange("p t v -> p v t"))
+            else:
+                nc.vector.tensor_copy(out_grouped[:], acc[:].rearrange("p t v -> p v t"))
+                nc.scalar.copy(result[:], acc[:])
+            quantize(out_codes[:, cols], out_scales[:, cols], out_grouped[:])
+            nc.sync.dma_start(words_out[:, cols], out_codes[:, cols].bitcast(I32))
+            nc.scalar.dma_start(out_rows[:, :, cols], result[:])
+
+        state = {}
+
+        def gather(s, d):
+            t, lo, n = steps[s]
+            g = sb(f"g{s}_{d}", [P, n], F32)
+            nc.vector.tensor_copy(g[:], e_rows[t][:].indirect(entries(pos_t[d], lo, n)))
+            state[(s, d)] = g
+
+        def larger(s, key, a, b):
+            n = steps[s][2]
+            m = sb(f"m{s}_{key}", [P, n], F32)
+            nc.vector.tensor_tensor(m[:], state[(s, a)][:], state[(s, b)][:], MAX)
+            state[(s, key)] = m
+
+        def add_centre(s):
+            t, lo, n = steps[s]
+            for c in range(0, n, HALF_V):
+                nc.vector.tensor_tensor(
+                    sums[(lo + c) // HALF_V][:, t, :],
+                    y_rows[t][:].indirect(entries(cen_t, lo + c, HALF_V)),
+                    state[(s, "all")][:, c : c + HALF_V],
+                    ADD,
+                )
+
+        for s in range(len(steps) + 1):
+            if s + 1 < PACK:
+                e_rows.append(hidden_rows("e", w2_raw, s + 1, 2 + s % 2))
+            if s < PACK:
+                y_rows.append(hidden_rows("y", w1_raw, s, 4 + s % 2))
+            if s == 2:
+                for part in range(4):
+                    w3_deal(part)
+                quantize(w3_codes[:], w3_scales[:], w3_grouped[:])
+            live, prev = s < len(steps), s > 0
+            if live:
+                gather(s, 0)
+            if prev:
+                larger(s - 1, "hi", 2, 3)
+            if live:
+                gather(s, 1)
+            if prev:
+                larger(s - 1, "all", "lo", "hi")
+            if live:
+                gather(s, 2)
+            if prev:
+                add_centre(s - 1)
+            if s == 4:
+                finish(0)
+            if live:
+                larger(s, "lo", 0, 1)
+                gather(s, 3)
+        finish(1)
+
+        scale_rows = out_2.rearrange("z q c -> (z q) c").bitcast(I32)
+        for quad in range(4):
+            queue = nc.sync if quad % 2 == 0 else nc.scalar
+            queue.dma_start(scale_rows[4 * quad : 4 * quad + 4, :], out_scales[32 * quad : 32 * quad + 4, :].bitcast(I32))

@@ -31,8 +31,8 @@ def tile_picked_edgecv_relu_lo_kernel(
         keep = ctx.enter_context(tc.tile_pool(name="keep", bufs=1))
         psum = ctx.enter_context(tc.psum_pool(name="psum", bufs=1))
 
-        def sb(name, shape, dtype):
-            return keep.tile(shape, dtype, name=name, align_bytes=64)
+        def sb(name, shape, dtype, tag=None):
+            return keep.tile(shape, dtype, name=name, tag=tag or name, align_bytes=64)
 
         def load_list(name, src):
             tile = keep.tile([P, src.shape[1]], U16, name=name)
@@ -69,46 +69,56 @@ def tile_picked_edgecv_relu_lo_kernel(
         nc.sync.dma_start(w1_raw[:], w1.rearrange("(p j) c -> p j c", j=PACK))
         cen_t = load_list("cen_t", cen)
         w3_raw = sb("w3_raw", [P, PACK, H], F32)
-        w3_rows = w3.rearrange("(b t q) c -> q b t c", t=PACK, q=8)
-        for q in (0, 4, 1, 5, 2, 6, 3, 7):
-            nc.sync.dma_start(w3_raw[q:P:8, :, :], w3_rows[q])
+        w3_rows = w3.rearrange("(b t q) c -> t b q c", t=PACK, q=8)
+        for t in range(PACK):
+            nc.sync.dma_start(w3_raw[:, t, :], w3_rows[t])
 
-        picked = [sb(f"picked{h}", [P, PACK, HALF_S], F32) for h in range(2)]
-        for j in range(PACK):
-            for h in range(2):
-                nc.vector.tensor_copy(picked[h][:, j, :], x_plane[j][:].indirect(entries(offs_t, h * HALF_S, HALF_S)))
+        picked_low = sb("picked_low", [P, 2, S], F32)
+        for j in range(2):
+            nc.vector.tensor_copy(picked_low[:, j, :], x_plane[j][:].indirect(offs_t[:]))
         x_grouped = [sb(f"x_grouped{h}", [P, HALF_S, PACK], BF16) for h in range(2)]
-        dst, src = weave_views(x_grouped[0][:], picked[0][:])
-        nc.scalar.copy(dst, src)
-        dst, src = weave_views(x_grouped[1][:], picked[1][:])
-        nc.vector.tensor_copy(dst, src)
+        picked_high = [sb(f"picked_high{h}", [P, 2, HALF_S], F32) for h in range(2)]
+        for h in range(2):
+            dst, src = weave_views(x_grouped[h][:, :, 0:2], picked_low[:, :, h * HALF_S : (h + 1) * HALF_S])
+            nc.scalar.copy(dst, src)
+        for j in range(2):
+            for h in range(2):
+                nc.vector.tensor_copy(picked_high[h][:, j, :], x_plane[2 + j][:].indirect(entries(offs_t, h * HALF_S, HALF_S)))
         x_codes = sb("x_codes", [P, S], U32)
         x_scales = sb("x_scales", [P, S], U8)
+        for h, copy in enumerate((nc.scalar.copy, nc.vector.tensor_copy)):
+            dst, src = weave_views(x_grouped[h][:, :, 2:4], picked_high[h][:])
+            copy(dst, src)
         for h in range(2):
             cols = slice(h * HALF_S, (h + 1) * HALF_S)
             quantize(x_codes[:, cols], x_scales[:, cols], x_grouped[h][:])
 
-        def hidden_weights(name, w_raw, t):
-            grouped = sb(f"{name}_grouped{t}", [P, P, PACK], BF16)
-            nc.scalar.copy(
-                grouped[:].rearrange("p (b u i) j -> p b u j i", u=2, i=4),
-                w_raw[:].rearrange("p j (b t u i) -> p t b u j i", t=PACK, u=2, i=4)[:, t],
-            )
-            codes = sb(f"{name}_codes{t}", [P, P], U32)
-            scales = sb(f"{name}_scales{t}", [P, P], U8)
+        def hidden_weights(name, parts, tag=None):
+            n = len(parts) * P
+            grouped = sb(f"{name}_grouped", [P, n, PACK], BF16, tag)
+            for k, (w_raw, t, copy) in enumerate(parts):
+                copy(
+                    grouped[:, k * P : (k + 1) * P, :].rearrange("p (b u i) j -> p b u j i", u=2, i=4),
+                    w_raw[:].rearrange("p j (b t u i) -> p t b u j i", t=PACK, u=2, i=4)[:, t],
+                )
+            codes = sb(f"{name}_codes", [P, n], U32)
+            scales = sb(f"{name}_scales", [P, n], U8)
             quantize(codes[:], scales[:], grouped[:])
             return codes, scales
 
-        def hidden_rows(name, w_raw, t, bank):
-            codes, scales = hidden_weights(name, w_raw, t)
-            acc = psum.tile([P, S], F32, name=f"{name}_acc{t}", tag=f"bank{bank}")
-            product(acc[:], codes[:], scales[:], x_codes[:], x_scales[:])
-            rows = sb(f"{name}_rows{t}", [P, S], F32)
-            nc.scalar.copy(rows[:], acc[:])
-            return rows
+        def hidden_rows(name, codes, scales, banks):
+            made = []
+            for k in range(len(banks)):
+                ms = slice(k * P, (k + 1) * P)
+                acc = psum.tile([P, S], F32, name=f"{name}_acc{k}", tag=f"bank{banks[k]}")
+                product(acc[:], codes[:, ms], scales[:, ms], x_codes[:], x_scales[:])
+                rows = sb(f"{name}_rows{k}", [P, S], F32)
+                nc.scalar.copy(rows[:], acc[:])
+                made.append(rows)
+            return made
 
-        codes, scales = hidden_weights("e", w2_raw, 0)
-        e_first = sb("e_rows0", [P, S], F32)
+        codes, scales = hidden_weights("e0", [(w2_raw, 0, nc.scalar.copy)], "w2_stage")
+        e_first = sb("e_first", [P, S], F32)
         for h in range(2):
             cols = slice(h * HALF_S, (h + 1) * HALF_S)
             acc = psum.tile([P, HALF_S], F32, name=f"e_first_acc{h}", tag=f"bank{h}")
@@ -117,107 +127,129 @@ def tile_picked_edgecv_relu_lo_kernel(
                 nc.scalar.copy(e_first[:, cols], acc[:])
             else:
                 nc.vector.tensor_copy(e_first[:, cols], acc[:])
-        e_rows = [e_first]
-        y_rows = []
+        e12 = hidden_weights("e12", [(w2_raw, t, nc.vector.tensor_copy) for t in (1, 2)], "w2_stage")
+        e3 = hidden_weights("e3", [(w2_raw, 3, nc.scalar.copy)])
+        e_rows = [e_first] + hidden_rows("e12", *e12, [2, 3]) + hidden_rows("e3", *e3, [4])
+        y_all = hidden_weights("y", [(w1_raw, t, nc.scalar.copy) for t in range(PACK)])
 
-        sums = [sb(f"sums{h}", [P, PACK, HALF_V], F32) for h in range(2)]
-        steps = [(0, 0, V), (1, 0, V), (2, 0, V), (3, 0, HALF_V), (3, HALF_V, HALF_V)]
+        sums = sb("sums", [P, PACK + 1, V], F32)
+        first, second = slice(0, HALF_V), slice(HALF_V, V)
 
-        w3_grouped = sb("w3_grouped", [P, H, PACK], BF16)
+        w3_grouped = sb("w3_grouped", [P, H, PACK], BF16, tag="shared")
         w3_codes = sb("w3_codes", [P, H], U32)
         w3_scales = sb("w3_scales", [P, H], U8)
 
         def w3_deal(part):
             ms = slice(32 * part, 32 * (part + 1))
             nc.scalar.copy(
-                w3_grouped[:].rearrange("p (t m) j -> p m j t", t=PACK)[:, ms],
-                w3_raw[:].rearrange("p j (m t) -> p m j t", t=PACK)[:, ms],
+                w3_grouped[:].rearrange("p (t m) j -> p m t j", t=PACK)[:, ms],
+                w3_raw[:].rearrange("p j (m t) -> p m t j", t=PACK)[:, ms],
             )
 
         out_codes = sb("out_codes", [P, V], U32)
         out_scales = sb("out_scales", [P, V], U8)
         out_rows = out_0.rearrange("(p t) v -> p t v", t=PACK)
         words_out = out_1.rearrange("z p c r -> p (z c r)").bitcast(I32)
+        z_grouped = [sb(f"z_grouped{h}", [P, HALF_V, PACK], BF16) for h in range(2)]
 
-        def finish(h):
-            cols = slice(h * HALF_V, (h + 1) * HALF_V)
-            z_grouped = sb(f"z_grouped{h}", [P, HALF_V, PACK], BF16)
-            dst, src = weave_views(z_grouped[:], sums[h][:])
-            if h == 0:
-                nc.scalar.activation(dst, src, RELU)
-            else:
-                nc.vector.tensor_scalar_max(dst, src, 0.0)
+        def quantize_z(h):
             z_codes = sb(f"z_codes{h}", [P, HALF_V], U32)
             z_scales = sb(f"z_scales{h}", [P, HALF_V], U8)
-            quantize(z_codes[:], z_scales[:], z_grouped[:])
-            acc = psum.tile([P, PACK, HALF_V], F32, name=f"out_acc{h}", tag=f"bank{6 + h}")
+            quantize(z_codes[:], z_scales[:], z_grouped[h][:])
+            return z_codes, z_scales
+
+        def project(acc, t, z_codes, z_scales):
+            ms = slice(t * P, (t + 1) * P)
+            product(acc, w3_codes[:, ms], w3_scales[:, ms], z_codes[:], z_scales[:])
+
+        def finish_first():
+            dst, src = weave_views(z_grouped[0][:, :, 2:4], sums[:, 2:4, first])
+            nc.vector.tensor_scalar_max(dst, src, 0.0)
+            z_codes, z_scales = quantize_z(0)
+            acc = psum.tile([P, PACK, HALF_V], F32, name="out_acc", tag="bank6")
             for t in range(PACK):
-                ms = slice(t * P, (t + 1) * P)
-                product(acc[:, t, :], w3_codes[:, ms], w3_scales[:, ms], z_codes[:], z_scales[:])
-            out_grouped = sb(f"out_grouped{h}", [P, HALF_V, PACK], BF16)
-            result = sb(f"result{h}", [P, PACK, HALF_V], F32)
-            if h == 0:
-                nc.scalar.copy(result[:], acc[:])
-                nc.scalar.copy(out_grouped[:], acc[:].rearrange("p t v -> p v t"))
-            else:
-                nc.vector.tensor_copy(out_grouped[:], acc[:].rearrange("p t v -> p v t"))
-                nc.scalar.copy(result[:], acc[:])
-            quantize(out_codes[:, cols], out_scales[:, cols], out_grouped[:])
-            nc.sync.dma_start(words_out[:, cols], out_codes[:, cols].bitcast(I32))
-            nc.scalar.dma_start(out_rows[:, :, cols], result[:])
+                project(acc[:, t, :], t, z_codes, z_scales)
+            out_grouped = sb("out_grouped0", [P, HALF_V, PACK], BF16)
+            result = sb("result0", [P, PACK, HALF_V], F32)
+            nc.scalar.copy(out_grouped[:], acc[:].rearrange("p t v -> p v t"))
+            nc.scalar.copy(result[:], acc[:])
+            quantize(out_codes[:, first], out_scales[:, first], out_grouped[:])
+            nc.sync.dma_start(words_out[:, first], out_codes[:, first].bitcast(I32))
+            nc.sync.dma_start(out_rows[:, :, first], result[:])
 
-        state = {}
+        def finish_second():
+            z_codes, z_scales = quantize_z(1)
+            out_grouped = sb("out_grouped1", [P, HALF_V, PACK], BF16)
+            accs = []
+            for u in range(2):
+                acc = psum.tile([P, 2, HALF_V], F32, name=f"out_pair_acc{u}", tag=f"bank{7 * (1 - u)}")
+                for e in range(2):
+                    project(acc[:, e, :], 2 * u + e, z_codes, z_scales)
+                accs.append(acc)
+            nc.scalar.copy(out_grouped[:, :, 0:2], accs[0][:].rearrange("p t v -> p v t"))
+            nc.vector.tensor_copy(out_grouped[:, :, 2:4], accs[1][:].rearrange("p t v -> p v t"))
+            quantize(out_codes[:, second], out_scales[:, second], out_grouped[:])
+            nc.sync.dma_start(words_out[:, second], out_codes[:, second].bitcast(I32))
+            result = sb("result1", [P, PACK, HALF_V], F32)
+            for u in range(2):
+                nc.scalar.copy(result[:, 2 * u : 2 * u + 2, :], accs[u][:])
+            nc.scalar.dma_start(out_rows[:, :, second], result[:])
 
-        def gather(s, d):
-            t, lo, n = steps[s]
-            g = sb(f"g{s}_{d}", [P, n], F32)
-            nc.vector.tensor_copy(g[:], e_rows[t][:].indirect(entries(pos_t[d], lo, n)))
-            state[(s, d)] = g
+        def gather(out, rows, lst, cols):
+            nc.vector.tensor_copy(out, rows[:].indirect(entries(lst, cols.start, cols.stop - cols.start)))
 
-        def larger(s, key, a, b):
-            n = steps[s][2]
-            m = sb(f"m{s}_{key}", [P, n], F32)
-            nc.vector.tensor_tensor(m[:], state[(s, a)][:], state[(s, b)][:], MAX)
-            state[(s, key)] = m
+        def gather_add(out, rows, lst, cols, other):
+            nc.vector.tensor_tensor(out, rows[:].indirect(entries(lst, cols.start, cols.stop - cols.start)), other, ADD)
 
-        def add_centre(s):
-            t, lo, n = steps[s]
-            for c in range(0, n, HALF_V):
-                nc.vector.tensor_tensor(
-                    sums[(lo + c) // HALF_V][:, t, :],
-                    y_rows[t][:].indirect(entries(cen_t, lo + c, HALF_V)),
-                    state[(s, "all")][:, c : c + HALF_V],
-                    ADD,
-                )
+        def step(t, cols):
+            n = cols.stop - cols.start
+            fetched = [sb(f"fetched{t}_{u}", [P, 2, n], F32) for u in range(2)]
+            for d in range(4):
+                gather(fetched[d % 2][:, d // 2, :], e_rows[t], pos_t[d], cols)
+            pairs = sb(f"pairs{t}", [P, 2, n], F32)
+            nc.vector.tensor_tensor(pairs[:], fetched[0][:], fetched[1][:], MAX)
+            largest = sb(f"largest{t}", [P, n], F32)
+            nc.vector.tensor_tensor(largest[:], pairs[:, 0, :], pairs[:, 1, :], MAX)
+            gather_add(sums[:, t, cols], y_rows[t], cen_t, cols, largest[:])
 
-        for s in range(len(steps) + 1):
-            if s + 1 < PACK:
-                e_rows.append(hidden_rows("e", w2_raw, s + 1, 2 + s % 2))
-            if s < PACK:
-                y_rows.append(hidden_rows("y", w1_raw, s, 4 + s % 2))
-            if s == 2:
-                for part in range(4):
-                    w3_deal(part)
-                quantize(w3_codes[:], w3_scales[:], w3_grouped[:])
-            live, prev = s < len(steps), s > 0
-            if live:
-                gather(s, 0)
-            if prev:
-                larger(s - 1, "hi", 2, 3)
-            if live:
-                gather(s, 1)
-            if prev:
-                larger(s - 1, "all", "lo", "hi")
-            if live:
-                gather(s, 2)
-            if prev:
-                add_centre(s - 1)
-            if s == 4:
-                finish(0)
-            if live:
-                larger(s, "lo", 0, 1)
-                gather(s, 3)
-        finish(1)
+        def last_step():
+            t = PACK - 1
+            part = sb("last", [P, 6, HALF_V], F32, tag="shared")
+            g0, g1, gy, low, a2, w = [part[:, i, :] for i in range(6)]
+            gather(g0, e_rows[t], pos_t[0], second)
+            gather(g1, e_rows[t], pos_t[1], second)
+            gather(gy, y_rows[t], cen_t, second)
+            nc.vector.tensor_tensor(low, g0, g1, MAX)
+            gather_add(a2, e_rows[t], pos_t[2], second, gy)
+            nc.vector.tensor_tensor(w, low, gy, ADD)
+            gather_add(sums[:, PACK, second], e_rows[t], pos_t[3], second, gy)
+            nc.vector.tensor_tensor(sums[:, t, second], w, a2, MAX)
+            nc.vector.scalar_tensor_tensor(
+                z_grouped[1][:, :, 2:4],
+                sums[:, 2:4, second].rearrange("p j v -> p v j"),
+                0.0,
+                sums[:, 2:5:2, second].rearrange("p j v -> p v j"),
+                MAX,
+                MAX,
+            )
+
+        everyone = slice(0, V)
+        for part in range(2):
+            w3_deal(part)
+        y_rows = hidden_rows("y", *y_all, [5, 0, 1, 2])
+        for part in range(2, 4):
+            w3_deal(part)
+        quantize(w3_codes[:], w3_scales[:], w3_grouped[:])
+        step(0, everyone)
+        step(1, everyone)
+        for h, cols in enumerate((first, second)):
+            dst, src = weave_views(z_grouped[h][:, :, 0:2], sums[:, 0:2, cols])
+            nc.scalar.activation(dst, src, RELU)
+        step(2, everyone)
+        step(3, first)
+        finish_first()
+        last_step()
+        finish_second()
 
         scale_rows = out_2.rearrange("z q c -> (z q) c").bitcast(I32)
         for quad in range(4):

@@ -29,6 +29,7 @@ def tile_picked_edgecv_relu_lo_kernel(
     nc = tc.nc
     with ExitStack() as ctx:
         keep = ctx.enter_context(tc.tile_pool(name="keep", bufs=1))
+        overlay = ctx.enter_context(tc.tile_pool(name="overlay", bufs=1))
         psum = ctx.enter_context(tc.psum_pool(name="psum", bufs=1))
 
         def sb(name, shape, dtype, tag=None):
@@ -68,7 +69,7 @@ def tile_picked_edgecv_relu_lo_kernel(
         w1_raw = sb("w1_raw", [P, PACK, H], F32)
         nc.sync.dma_start(w1_raw[:], w1.rearrange("(p j) c -> p j c", j=PACK))
         cen_t = load_list("cen_t", cen)
-        w3_raw = sb("w3_raw", [P, PACK, H], F32)
+        w3_raw = overlay.tile([P, PACK, H], F32, name="w3_raw", offset=0)
         w3_rows = w3.rearrange("(b t q) c -> t b q c", t=PACK, q=8)
         for t in range(PACK):
             nc.sync.dma_start(w3_raw[:, t, :], w3_rows[t])
@@ -106,13 +107,16 @@ def tile_picked_edgecv_relu_lo_kernel(
             quantize(codes[:], scales[:], grouped[:])
             return codes, scales
 
-        def hidden_rows(name, codes, scales, banks):
+        def hidden_rows(name, codes, scales, banks, shared=False):
             made = []
             for k in range(len(banks)):
                 ms = slice(k * P, (k + 1) * P)
                 acc = psum.tile([P, S], F32, name=f"{name}_acc{k}", tag=f"bank{banks[k]}")
                 product(acc[:], codes[:, ms], scales[:, ms], x_codes[:], x_scales[:])
-                rows = sb(f"{name}_rows{k}", [P, S], F32)
+                if shared:
+                    rows = overlay.tile([P, S], F32, name=f"{name}_rows{k}", offset=4 * S * k)
+                else:
+                    rows = sb(f"{name}_rows{k}", [P, S], F32)
                 nc.scalar.copy(rows[:], acc[:])
                 made.append(rows)
             return made
@@ -135,7 +139,7 @@ def tile_picked_edgecv_relu_lo_kernel(
         sums = sb("sums", [P, PACK + 1, V], F32)
         first, second = slice(0, HALF_V), slice(HALF_V, V)
 
-        w3_grouped = sb("w3_grouped", [P, H, PACK], BF16, tag="shared")
+        w3_grouped = sb("w3_grouped", [P, H, PACK], BF16)
         w3_codes = sb("w3_codes", [P, H], U32)
         w3_scales = sb("w3_scales", [P, H], U8)
 
@@ -214,7 +218,7 @@ def tile_picked_edgecv_relu_lo_kernel(
 
         def last_step():
             t = PACK - 1
-            part = sb("last", [P, 6, HALF_V], F32, tag="shared")
+            part = overlay.tile([P, 6, HALF_V], F32, name="last", offset=4 * S)
             g0, g1, gy, low, a2, w = [part[:, i, :] for i in range(6)]
             gather(g0, e_rows[t], pos_t[0], second)
             gather(g1, e_rows[t], pos_t[1], second)
@@ -234,11 +238,9 @@ def tile_picked_edgecv_relu_lo_kernel(
             )
 
         everyone = slice(0, V)
-        for part in range(2):
+        for part in range(4):
             w3_deal(part)
-        y_rows = hidden_rows("y", *y_all, [5, 0, 1, 2])
-        for part in range(2, 4):
-            w3_deal(part)
+        y_rows = hidden_rows("y", *y_all, [5, 0, 1, 2], True)
         quantize(w3_codes[:], w3_scales[:], w3_grouped[:])
         step(0, everyone)
         step(1, everyone)

@@ -1,6 +1,7 @@
 from contextlib import ExitStack
 
 import concourse.mybir as mybir
+from concourse.masks import make_identity
 
 K, T, S, V, H = 512, 1024, 512, 256, 512
 FLOPS = 2 * (2 * K * H * S + H * H * V)
@@ -58,6 +59,14 @@ def tile_picked_edgecv_relu_lo_kernel(
                 planes.rearrange("p j (c i) -> p c j i", i=4),
             )
 
+        def laid(name, shape, dtype, kib):
+            return overlay.tile(shape, dtype, name=name, offset=1024 * kib, align_bytes=64)
+
+        ident_f32 = sb("ident_f32", [P, P], F32)
+        make_identity(nc, ident_f32[:])
+        ident_bf16 = sb("ident_bf16", [P, P], BF16)
+        make_identity(nc, ident_bf16[:])
+
         offs_t = load_list("offs_t", offs)
         x_rows = xT.rearrange("(p j) c -> j p c", j=PACK)
         x_plane = [sb(f"x_plane{j}", [P, T], F32) for j in range(PACK)]
@@ -69,7 +78,7 @@ def tile_picked_edgecv_relu_lo_kernel(
         w1_raw = sb("w1_raw", [P, PACK, H], F32)
         nc.sync.dma_start(w1_raw[:], w1.rearrange("(p j) c -> p j c", j=PACK))
         cen_t = load_list("cen_t", cen)
-        w3_raw = overlay.tile([P, PACK, H], F32, name="w3_raw", offset=0)
+        w3_raw = laid("w3_raw", [P, PACK, H], F32, 0)
         w3_rows = w3.rearrange("(b t q) c -> t b q c", t=PACK, q=8)
         for t in range(PACK):
             nc.sync.dma_start(w3_raw[:, t, :], w3_rows[t])
@@ -94,9 +103,12 @@ def tile_picked_edgecv_relu_lo_kernel(
             cols = slice(h * HALF_S, (h + 1) * HALF_S)
             quantize(x_codes[:, cols], x_scales[:, cols], x_grouped[h][:])
 
-        def hidden_weights(name, parts, tag=None):
+        def hidden_weights(name, parts, tag=None, kib=None):
             n = len(parts) * P
-            grouped = sb(f"{name}_grouped", [P, n, PACK], BF16, tag)
+            if kib is None:
+                grouped = sb(f"{name}_grouped", [P, n, PACK], BF16, tag)
+            else:
+                grouped = laid(f"{name}_grouped", [P, n, PACK], BF16, kib)
             for k, (w_raw, t, copy) in enumerate(parts):
                 copy(
                     grouped[:, k * P : (k + 1) * P, :].rearrange("p (b u i) j -> p b u j i", u=2, i=4),
@@ -107,14 +119,14 @@ def tile_picked_edgecv_relu_lo_kernel(
             quantize(codes[:], scales[:], grouped[:])
             return codes, scales
 
-        def hidden_rows(name, codes, scales, banks, shared=False):
+        def hidden_rows(name, codes, scales, banks, kibs=None):
             made = []
             for k in range(len(banks)):
                 ms = slice(k * P, (k + 1) * P)
                 acc = psum.tile([P, S], F32, name=f"{name}_acc{k}", tag=f"bank{banks[k]}")
                 product(acc[:], codes[:, ms], scales[:, ms], x_codes[:], x_scales[:])
-                if shared:
-                    rows = overlay.tile([P, S], F32, name=f"{name}_rows{k}", offset=4 * S * k)
+                if kibs:
+                    rows = laid(f"{name}_rows{k}", [P, S], F32, kibs[k])
                 else:
                     rows = sb(f"{name}_rows{k}", [P, S], F32)
                 nc.scalar.copy(rows[:], acc[:])
@@ -133,8 +145,10 @@ def tile_picked_edgecv_relu_lo_kernel(
                 nc.vector.tensor_copy(e_first[:, cols], acc[:])
         e12 = hidden_weights("e12", [(w2_raw, t, nc.vector.tensor_copy) for t in (1, 2)], "w2_stage")
         e3 = hidden_weights("e3", [(w2_raw, 3, nc.scalar.copy)])
+        y01 = hidden_weights("y01", [(w1_raw, t, nc.scalar.copy) for t in (0, 1)], None, 14)
         e_rows = [e_first] + hidden_rows("e12", *e12, [2, 3]) + hidden_rows("e3", *e3, [4])
-        y_all = hidden_weights("y", [(w1_raw, t, nc.scalar.copy) for t in range(PACK)])
+        y_rows = hidden_rows("y01", *y01, [5, 0], [8, 12])
+        y23 = hidden_weights("y23", [(w1_raw, t, nc.scalar.copy) for t in (2, 3)])
 
         sums = sb("sums", [P, PACK + 1, V], F32)
         first, second = slice(0, HALF_V), slice(HALF_V, V)
@@ -170,34 +184,35 @@ def tile_picked_edgecv_relu_lo_kernel(
             dst, src = weave_views(z_grouped[0][:, :, 2:4], sums[:, 2:4, first])
             nc.vector.tensor_scalar_max(dst, src, 0.0)
             z_codes, z_scales = quantize_z(0)
-            acc = psum.tile([P, PACK, HALF_V], F32, name="out_acc", tag="bank6")
+            acc = psum.tile([P, PACK, HALF_V], F32, name="out_acc", tag="bank3")
             for t in range(PACK):
                 project(acc[:, t, :], t, z_codes, z_scales)
             out_grouped = sb("out_grouped0", [P, HALF_V, PACK], BF16)
             result = sb("result0", [P, PACK, HALF_V], F32)
             nc.scalar.copy(out_grouped[:], acc[:].rearrange("p t v -> p v t"))
             nc.scalar.copy(result[:], acc[:])
+            nc.sync.dma_start(out_rows[:, :, first], result[:])
             quantize(out_codes[:, first], out_scales[:, first], out_grouped[:])
             nc.sync.dma_start(words_out[:, first], out_codes[:, first].bitcast(I32))
-            nc.sync.dma_start(out_rows[:, :, first], result[:])
 
         def finish_second():
             z_codes, z_scales = quantize_z(1)
             out_grouped = sb("out_grouped1", [P, HALF_V, PACK], BF16)
             accs = []
             for u in range(2):
-                acc = psum.tile([P, 2, HALF_V], F32, name=f"out_pair_acc{u}", tag=f"bank{7 * (1 - u)}")
+                acc = psum.tile([P, 2, HALF_V], F32, name=f"out_pair_acc{u}", tag=f"bank{4 * (1 - u)}")
                 for e in range(2):
                     project(acc[:, e, :], 2 * u + e, z_codes, z_scales)
                 accs.append(acc)
             nc.scalar.copy(out_grouped[:, :, 0:2], accs[0][:].rearrange("p t v -> p v t"))
             nc.vector.tensor_copy(out_grouped[:, :, 2:4], accs[1][:].rearrange("p t v -> p v t"))
+            results = [sb(f"result_pair{u}", [P, 2, HALF_V], F32) for u in range(2)]
+            nc.scalar.copy(results[0][:], accs[0][:])
+            nc.vector.tensor_copy(results[1][:], accs[1][:])
+            nc.scalar.dma_start(out_rows[:, 0:2, second], results[0][:])
+            nc.sync.dma_start(out_rows[:, 2:4, second], results[1][:])
             quantize(out_codes[:, second], out_scales[:, second], out_grouped[:])
             nc.sync.dma_start(words_out[:, second], out_codes[:, second].bitcast(I32))
-            result = sb("result1", [P, PACK, HALF_V], F32)
-            for u in range(2):
-                nc.scalar.copy(result[:, 2 * u : 2 * u + 2, :], accs[u][:])
-            nc.scalar.dma_start(out_rows[:, :, second], result[:])
 
         def gather(out, rows, lst, cols):
             nc.vector.tensor_copy(out, rows[:].indirect(entries(lst, cols.start, cols.stop - cols.start)))
@@ -205,20 +220,42 @@ def tile_picked_edgecv_relu_lo_kernel(
         def gather_add(out, rows, lst, cols, other):
             nc.vector.tensor_tensor(out, rows[:].indirect(entries(lst, cols.start, cols.stop - cols.start)), other, ADD)
 
-        def step(t, cols):
-            n = cols.stop - cols.start
-            fetched = [sb(f"fetched{t}_{u}", [P, 2, n], F32) for u in range(2)]
+        turned_back = psum.tile([P, 2, 2, HALF_V], BF16, name="turned_back", tag="bank5")
+
+        def fetch(t, cols, fetched):
             for d in range(4):
-                gather(fetched[d % 2][:, d // 2, :], e_rows[t], pos_t[d], cols)
+                gather(fetched[d], e_rows[t], pos_t[d], cols)
+
+        def turned_step(t, fetched, banks):
+            centre = sb(f"centre{t}", [P, V], F32)
+            gather(centre[:], y_rows[t], cen_t, everyone)
+            edges = laid(f"edges{t}", [P, 2, 4, P], BF16, 2 * t)
+            for h, cols in enumerate((first, second)):
+                acc = psum.tile([P, 4, P], F32, name=f"edge_acc{t}_{h}", tag=f"bank{banks[h]}")
+                for d in range(4):
+                    nc.tensor.matmul(acc[:, d, :], fetched[d][:, cols], ident_f32[:], start=True, stop=False, is_transpose=True)
+                    nc.tensor.matmul(acc[:, d, :], centre[:, cols], ident_f32[:], start=False, stop=True, is_transpose=True)
+                nc.scalar.activation(edges[:, h, :, :], acc[:], RELU)
+            pairs = sb(f"edge_pairs{t}", [P, 2, 2, P], BF16)
+            nc.vector.tensor_tensor(pairs[:], edges[:, :, 0:2, :], edges[:, :, 2:4, :], MAX)
+            largest = sb(f"edge_largest{t}", [P, 2, P], BF16)
+            nc.vector.tensor_tensor(largest[:], pairs[:, :, 0, :], pairs[:, :, 1, :], MAX)
+            for h in range(2):
+                nc.tensor.transpose(turned_back[:, h, t, :], largest[:, h, :], ident_bf16[:])
+
+        def step(t, cols, kib):
+            n = cols.stop - cols.start
+            fetched = laid(f"fetched{t}", [P, 4, n], F32, kib)
+            fetch(t, cols, [fetched[:, d, :] for d in range(4)])
             pairs = sb(f"pairs{t}", [P, 2, n], F32)
-            nc.vector.tensor_tensor(pairs[:], fetched[0][:], fetched[1][:], MAX)
+            nc.vector.tensor_tensor(pairs[:], fetched[:, 0:2, :], fetched[:, 2:4, :], MAX)
             largest = sb(f"largest{t}", [P, n], F32)
             nc.vector.tensor_tensor(largest[:], pairs[:, 0, :], pairs[:, 1, :], MAX)
             gather_add(sums[:, t, cols], y_rows[t], cen_t, cols, largest[:])
 
         def last_step():
             t = PACK - 1
-            part = overlay.tile([P, 6, HALF_V], F32, name="last", offset=4 * S)
+            part = laid("last", [P, 6, HALF_V], F32, 3)
             g0, g1, gy, low, a2, w = [part[:, i, :] for i in range(6)]
             gather(g0, e_rows[t], pos_t[0], second)
             gather(g1, e_rows[t], pos_t[1], second)
@@ -240,15 +277,20 @@ def tile_picked_edgecv_relu_lo_kernel(
         everyone = slice(0, V)
         for part in range(4):
             w3_deal(part)
-        y_rows = hidden_rows("y", *y_all, [5, 0, 1, 2], True)
         quantize(w3_codes[:], w3_scales[:], w3_grouped[:])
-        step(0, everyone)
-        step(1, everyone)
-        for h, cols in enumerate((first, second)):
-            dst, src = weave_views(z_grouped[h][:, :, 0:2], sums[:, 0:2, cols])
-            nc.scalar.activation(dst, src, RELU)
-        step(2, everyone)
-        step(3, first)
+        early = sb("early", [P, 6, V], F32)
+        held = laid("held", [P, 2, V], F32, 14)
+        fetched0 = [early[:, d, :] for d in range(4)]
+        fetched1 = [early[:, 4, :], early[:, 5, :], held[:, 0, :], held[:, 1, :]]
+        fetch(0, everyone, fetched0)
+        fetch(1, everyone, fetched1)
+        turned_step(0, fetched0, [3, 4])
+        turned_step(1, fetched1, [6, 7])
+        y_rows.extend(hidden_rows("y23", *y23, [1, 2], [4, 6]))
+        for h in range(2):
+            nc.scalar.copy(z_grouped[h][:, :, 0:2], turned_back[:, h, :, :].rearrange("p t v -> p v t"))
+        step(2, everyone, 8)
+        step(3, first, 0)
         finish_first()
         last_step()
         finish_second()

@@ -19,9 +19,23 @@ RELU = mybir.ActivationFunctionType.Relu
 
 P = 128
 PACK = 4
+NEIGHBOURS = 4
 LIST_ROWS = 16
+BLOCK_ROWS = 8
+LINE = 4
+DEAL_PARTS = 4
 HALF_S = S // 2
 HALF_V = V // 2
+LOW, HIGH = slice(0, 2), slice(2, 4)
+
+W3_RAW_AT = 0
+EDGES_AT = (0, 2)
+Y_LATE_AT = (4, 6)
+TILE3_FETCH_AT = 0
+LAST_AT = 3
+Y_EARLY_AT = (8, 12)
+TILE2_FETCH_AT = 8
+Y_STAGE_AT = 14
 
 
 def tile_picked_edgecv_relu_lo_kernel(
@@ -36,31 +50,45 @@ def tile_picked_edgecv_relu_lo_kernel(
         def sb(name, shape, dtype, tag=None):
             return keep.tile(shape, dtype, name=name, tag=tag or name, align_bytes=64)
 
-        def load_list(name, src):
-            tile = keep.tile([P, src.shape[1]], U16, name=name)
-            nc.sync.dma_start(tile[:], src)
+        def laid(name, shape, dtype, kib):
+            return overlay.tile(shape, dtype, name=name, offset=1024 * kib, align_bytes=64)
+
+        def bank(name, shape, dtype, number):
+            return psum.tile(shape, dtype, name=name, tag=f"bank{number}")
+
+        def load_list(name, source):
+            tile = keep.tile([P, source.shape[1]], U16, name=name)
+            nc.sync.dma_start(tile[:], source)
             return tile
 
-        def entries(lst, lo, n):
-            return lst[:, lo // LIST_ROWS : (lo + n) // LIST_ROWS]
+        def looked_up(rows, list_tile, cols):
+            return rows[:].indirect(list_tile[:, cols.start // LIST_ROWS : cols.stop // LIST_ROWS])
+
+        def gather(out, rows, list_tile, cols):
+            nc.vector.tensor_copy(out, looked_up(rows, list_tile, cols))
+
+        def gather_add(out, rows, list_tile, cols, other):
+            nc.vector.tensor_tensor(out, looked_up(rows, list_tile, cols), other, ADD)
 
         def quantize(codes, scales, grouped):
             nc.vector.quantize_mx(out=codes.bitcast(FP8X4), scales=scales, in_=grouped.rearrange("p c j -> p (c j)"))
 
-        def product(acc, w_codes, w_scales, x_codes, x_scales):
+        def product(acc, w_codes, w_scales, moving_codes, moving_scales):
             nc.tensor.matmul_mx(
-                out=acc, lhsT=w_codes.bitcast(FP8X4), lhsT_scale=w_scales,
-                rhs=x_codes.bitcast(FP8X4), rhs_scale=x_scales, start=True, stop=True,
+                out=acc,
+                lhsT=w_codes.bitcast(FP8X4),
+                lhsT_scale=w_scales,
+                rhs=moving_codes.bitcast(FP8X4),
+                rhs_scale=moving_scales,
+                start=True,
+                stop=True,
             )
 
         def weave_views(grouped, planes):
             return (
-                grouped.rearrange("p (c i) j -> p c j i", i=4),
-                planes.rearrange("p j (c i) -> p c j i", i=4),
+                grouped.rearrange("p (c i) j -> p c j i", i=LINE),
+                planes.rearrange("p j (c i) -> p c j i", i=LINE),
             )
-
-        def laid(name, shape, dtype, kib):
-            return overlay.tile(shape, dtype, name=name, offset=1024 * kib, align_bytes=64)
 
         ident_f32 = sb("ident_f32", [P, P], F32)
         make_identity(nc, ident_f32[:])
@@ -74,101 +102,150 @@ def tile_picked_edgecv_relu_lo_kernel(
             nc.sync.dma_start(x_plane[j][:], x_rows[j])
         w2_raw = sb("w2_raw", [P, PACK, H], F32)
         nc.sync.dma_start(w2_raw[:], w2.rearrange("(p j) c -> p j c", j=PACK))
-        pos_t = [load_list(f"pos{d}_t", src) for d, src in enumerate((pos1, pos2, pos3, pos4))]
+        pos_t = [load_list(f"pos{d}_t", source) for d, source in enumerate((pos1, pos2, pos3, pos4))]
         w1_raw = sb("w1_raw", [P, PACK, H], F32)
         nc.sync.dma_start(w1_raw[:], w1.rearrange("(p j) c -> p j c", j=PACK))
         cen_t = load_list("cen_t", cen)
-        w3_raw = laid("w3_raw", [P, PACK, H], F32, 0)
-        w3_rows = w3.rearrange("(b t q) c -> t b q c", t=PACK, q=8)
+        w3_raw = laid("w3_raw", [P, PACK, H], F32, W3_RAW_AT)
+        w3_rows = w3.rearrange("(b t q) c -> t b q c", t=PACK, q=BLOCK_ROWS)
         for t in range(PACK):
             nc.sync.dma_start(w3_raw[:, t, :], w3_rows[t])
 
+        point_halves = (slice(0, HALF_S), slice(HALF_S, S))
         picked_low = sb("picked_low", [P, 2, S], F32)
         for j in range(2):
             nc.vector.tensor_copy(picked_low[:, j, :], x_plane[j][:].indirect(offs_t[:]))
         x_grouped = [sb(f"x_grouped{h}", [P, HALF_S, PACK], BF16) for h in range(2)]
         picked_high = [sb(f"picked_high{h}", [P, 2, HALF_S], F32) for h in range(2)]
-        for h in range(2):
-            dst, src = weave_views(x_grouped[h][:, :, 0:2], picked_low[:, :, h * HALF_S : (h + 1) * HALF_S])
-            nc.scalar.copy(dst, src)
+        for h, points in enumerate(point_halves):
+            nc.scalar.copy(*weave_views(x_grouped[h][:, :, LOW], picked_low[:, :, points]))
         for j in range(2):
-            for h in range(2):
-                nc.vector.tensor_copy(picked_high[h][:, j, :], x_plane[2 + j][:].indirect(entries(offs_t, h * HALF_S, HALF_S)))
+            for h, points in enumerate(point_halves):
+                gather(picked_high[h][:, j, :], x_plane[2 + j], offs_t, points)
         x_codes = sb("x_codes", [P, S], U32)
         x_scales = sb("x_scales", [P, S], U8)
         for h, copy in enumerate((nc.scalar.copy, nc.vector.tensor_copy)):
-            dst, src = weave_views(x_grouped[h][:, :, 2:4], picked_high[h][:])
-            copy(dst, src)
-        for h in range(2):
-            cols = slice(h * HALF_S, (h + 1) * HALF_S)
-            quantize(x_codes[:, cols], x_scales[:, cols], x_grouped[h][:])
+            copy(*weave_views(x_grouped[h][:, :, HIGH], picked_high[h][:]))
+        for h, points in enumerate(point_halves):
+            quantize(x_codes[:, points], x_scales[:, points], x_grouped[h][:])
 
-        def hidden_weights(name, parts, tag=None, kib=None):
-            n = len(parts) * P
-            if kib is None:
-                grouped = sb(f"{name}_grouped", [P, n, PACK], BF16, tag)
-            else:
-                grouped = laid(f"{name}_grouped", [P, n, PACK], BF16, kib)
-            for k, (w_raw, t, copy) in enumerate(parts):
+        def stage_shape(tiles):
+            return [P, len(tiles) * P, PACK]
+
+        def hidden_weights(name, w_raw, tiles, copy, grouped):
+            for n, t in enumerate(tiles):
                 copy(
-                    grouped[:, k * P : (k + 1) * P, :].rearrange("p (b u i) j -> p b u j i", u=2, i=4),
-                    w_raw[:].rearrange("p j (b t u i) -> p t b u j i", t=PACK, u=2, i=4)[:, t],
+                    grouped[:, n * P : (n + 1) * P, :].rearrange("p (b u i) j -> p b u j i", u=2, i=LINE),
+                    w_raw[:].rearrange("p j (b t u i) -> p t b u j i", t=PACK, u=2, i=LINE)[:, t],
                 )
-            codes = sb(f"{name}_codes", [P, n], U32)
-            scales = sb(f"{name}_scales", [P, n], U8)
+            codes = sb(f"{name}_codes", [P, len(tiles) * P], U32)
+            scales = sb(f"{name}_scales", [P, len(tiles) * P], U8)
             quantize(codes[:], scales[:], grouped[:])
             return codes, scales
 
-        def hidden_rows(name, codes, scales, banks, kibs=None):
+        def hidden_rows(name, weights, banks, make_rows):
+            codes, scales = weights
             made = []
-            for k in range(len(banks)):
-                ms = slice(k * P, (k + 1) * P)
-                acc = psum.tile([P, S], F32, name=f"{name}_acc{k}", tag=f"bank{banks[k]}")
-                product(acc[:], codes[:, ms], scales[:, ms], x_codes[:], x_scales[:])
-                if kibs:
-                    rows = laid(f"{name}_rows{k}", [P, S], F32, kibs[k])
-                else:
-                    rows = sb(f"{name}_rows{k}", [P, S], F32)
+            for n, number in enumerate(banks):
+                place = slice(n * P, (n + 1) * P)
+                acc = bank(f"{name}_acc{n}", [P, S], F32, number)
+                product(acc[:], codes[:, place], scales[:, place], x_codes[:], x_scales[:])
+                rows = make_rows(f"{name}_rows{n}", n)
                 nc.scalar.copy(rows[:], acc[:])
                 made.append(rows)
             return made
 
-        codes, scales = hidden_weights("e0", [(w2_raw, 0, nc.scalar.copy)], "w2_stage")
-        e_first = sb("e_first", [P, S], F32)
-        for h in range(2):
-            cols = slice(h * HALF_S, (h + 1) * HALF_S)
-            acc = psum.tile([P, HALF_S], F32, name=f"e_first_acc{h}", tag=f"bank{h}")
-            product(acc[:], codes[:], scales[:], x_codes[:, cols], x_scales[:, cols])
-            if h == 0:
-                nc.scalar.copy(e_first[:, cols], acc[:])
-            else:
-                nc.vector.tensor_copy(e_first[:, cols], acc[:])
-        e12 = hidden_weights("e12", [(w2_raw, t, nc.vector.tensor_copy) for t in (1, 2)], "w2_stage")
-        e3 = hidden_weights("e3", [(w2_raw, 3, nc.scalar.copy)])
-        y01 = hidden_weights("y01", [(w1_raw, t, nc.scalar.copy) for t in (0, 1)], None, 14)
-        e_rows = [e_first] + hidden_rows("e12", *e12, [2, 3]) + hidden_rows("e3", *e3, [4])
-        y_rows = hidden_rows("y01", *y01, [5, 0], [8, 12])
-        y23 = hidden_weights("y23", [(w1_raw, t, nc.scalar.copy) for t in (2, 3)])
+        def own_rows(name, n):
+            return sb(name, [P, S], F32)
 
-        sums = sb("sums", [P, PACK + 1, V], F32)
-        first, second = slice(0, HALF_V), slice(HALF_V, V)
+        def rows_at(kibs):
+            return lambda name, n: laid(name, [P, S], F32, kibs[n])
+
+        e0_stage = sb("e0_grouped", stage_shape([0]), BF16, "w2_stage")
+        e0_codes, e0_scales = hidden_weights("e0", w2_raw, [0], nc.scalar.copy, e0_stage)
+        e_first = sb("e_first", [P, S], F32)
+        for h, copy in enumerate((nc.scalar.copy, nc.vector.tensor_copy)):
+            points = point_halves[h]
+            acc = bank(f"e_first_acc{h}", [P, HALF_S], F32, h)
+            product(acc[:], e0_codes[:], e0_scales[:], x_codes[:, points], x_scales[:, points])
+            copy(e_first[:, points], acc[:])
+        e12_stage = sb("e12_grouped", stage_shape([1, 2]), BF16, "w2_stage")
+        e12 = hidden_weights("e12", w2_raw, [1, 2], nc.vector.tensor_copy, e12_stage)
+        e3 = hidden_weights("e3", w2_raw, [3], nc.scalar.copy, sb("e3_grouped", stage_shape([3]), BF16))
+        y01_stage = laid("y01_grouped", stage_shape([0, 1]), BF16, Y_STAGE_AT)
+        y01 = hidden_weights("y01", w1_raw, [0, 1], nc.scalar.copy, y01_stage)
+        e_rows = [e_first] + hidden_rows("e12", e12, [2, 3], own_rows) + hidden_rows("e3", e3, [4], own_rows)
+        y_rows = hidden_rows("y01", y01, [5, 0], rows_at(Y_EARLY_AT))
+        y23 = hidden_weights("y23", w1_raw, [2, 3], nc.scalar.copy, sb("y23_grouped", stage_shape([2, 3]), BF16))
+
+        sums = sb("sums", [P, 3, V], F32)
+        first, second, everyone = slice(0, HALF_V), slice(HALF_V, V), slice(0, V)
 
         w3_grouped = sb("w3_grouped", [P, H, PACK], BF16)
         w3_codes = sb("w3_codes", [P, H], U32)
         w3_scales = sb("w3_scales", [P, H], U8)
-
-        def w3_deal(part):
-            ms = slice(32 * part, 32 * (part + 1))
-            nc.scalar.copy(
-                w3_grouped[:].rearrange("p (t m) j -> p m t j", t=PACK)[:, ms],
-                w3_raw[:].rearrange("p j (m t) -> p m t j", t=PACK)[:, ms],
-            )
-
         out_codes = sb("out_codes", [P, V], U32)
         out_scales = sb("out_scales", [P, V], U8)
         out_rows = out_0.rearrange("(p t) v -> p t v", t=PACK)
         words_out = out_1.rearrange("z p c r -> p (z c r)").bitcast(I32)
         z_grouped = [sb(f"z_grouped{h}", [P, HALF_V, PACK], BF16) for h in range(2)]
+        turned_back = bank("turned_back", [P, 2, 2, HALF_V], BF16, 5)
+
+        def fetch(t, cols, fetched):
+            for d in range(NEIGHBOURS):
+                gather(fetched[d], e_rows[t], pos_t[d], cols)
+
+        def turned_step(t, fetched, banks):
+            centre = sb(f"centre{t}", [P, V], F32)
+            gather(centre[:], y_rows[t], cen_t, everyone)
+            edges = laid(f"edges{t}", [P, 2, NEIGHBOURS, P], BF16, EDGES_AT[t])
+            for h, cols in enumerate((first, second)):
+                acc = bank(f"edge_acc{t}_{h}", [P, NEIGHBOURS, P], F32, banks[h])
+                for d in range(NEIGHBOURS):
+                    nc.tensor.matmul(
+                        acc[:, d, :], fetched[d][:, cols], ident_f32[:], start=True, stop=False, is_transpose=True
+                    )
+                    nc.tensor.matmul(
+                        acc[:, d, :], centre[:, cols], ident_f32[:], start=False, stop=True, is_transpose=True
+                    )
+                nc.scalar.activation(edges[:, h, :, :], acc[:], RELU)
+            pairs = sb(f"edge_pairs{t}", [P, 2, 2, P], BF16)
+            nc.vector.tensor_tensor(pairs[:], edges[:, :, 0:2, :], edges[:, :, 2:4, :], MAX)
+            largest = sb(f"edge_largest{t}", [P, 2, P], BF16)
+            nc.vector.tensor_tensor(largest[:], pairs[:, :, 0, :], pairs[:, :, 1, :], MAX)
+            for h in range(2):
+                nc.tensor.transpose(turned_back[:, h, t, :], largest[:, h, :], ident_bf16[:])
+
+        def vector_step(t, cols, kib):
+            n = cols.stop - cols.start
+            fetched = laid(f"fetched{t}", [P, NEIGHBOURS, n], F32, kib)
+            fetch(t, cols, [fetched[:, d, :] for d in range(NEIGHBOURS)])
+            pairs = sb(f"pairs{t}", [P, 2, n], F32)
+            nc.vector.tensor_tensor(pairs[:], fetched[:, 0:2, :], fetched[:, 2:4, :], MAX)
+            largest = sb(f"largest{t}", [P, n], F32)
+            nc.vector.tensor_tensor(largest[:], pairs[:, 0, :], pairs[:, 1, :], MAX)
+            gather_add(sums[:, t - 2, cols], y_rows[t], cen_t, cols, largest[:])
+
+        def last_step():
+            t = PACK - 1
+            part = laid("last", [P, 6, HALF_V], F32, LAST_AT)
+            near0, near1, centre, larger, edge2, edge01 = [part[:, n, :] for n in range(6)]
+            gather(near0, e_rows[t], pos_t[0], second)
+            gather(near1, e_rows[t], pos_t[1], second)
+            gather(centre, y_rows[t], cen_t, second)
+            nc.vector.tensor_tensor(larger, near0, near1, MAX)
+            gather_add(edge2, e_rows[t], pos_t[2], second, centre)
+            nc.vector.tensor_tensor(edge01, larger, centre, ADD)
+            gather_add(sums[:, 2, second], e_rows[t], pos_t[3], second, centre)
+            nc.vector.tensor_tensor(sums[:, 1, second], edge01, edge2, MAX)
+            nc.vector.scalar_tensor_tensor(
+                z_grouped[1][:, :, HIGH],
+                sums[:, 0:2, second].rearrange("p j v -> p v j"),
+                0.0,
+                sums[:, 0:3:2, second].rearrange("p j v -> p v j"),
+                MAX,
+                MAX,
+            )
 
         def quantize_z(h):
             z_codes = sb(f"z_codes{h}", [P, HALF_V], U32)
@@ -177,14 +254,14 @@ def tile_picked_edgecv_relu_lo_kernel(
             return z_codes, z_scales
 
         def project(acc, t, z_codes, z_scales):
-            ms = slice(t * P, (t + 1) * P)
-            product(acc, w3_codes[:, ms], w3_scales[:, ms], z_codes[:], z_scales[:])
+            place = slice(t * P, (t + 1) * P)
+            product(acc, w3_codes[:, place], w3_scales[:, place], z_codes[:], z_scales[:])
 
         def finish_first():
-            dst, src = weave_views(z_grouped[0][:, :, 2:4], sums[:, 2:4, first])
-            nc.vector.tensor_scalar_max(dst, src, 0.0)
+            woven, planes = weave_views(z_grouped[0][:, :, HIGH], sums[:, 0:2, first])
+            nc.scalar.activation(woven, planes, RELU)
             z_codes, z_scales = quantize_z(0)
-            acc = psum.tile([P, PACK, HALF_V], F32, name="out_acc", tag="bank3")
+            acc = bank("out_acc", [P, PACK, HALF_V], F32, 3)
             for t in range(PACK):
                 project(acc[:, t, :], t, z_codes, z_scales)
             out_grouped = sb("out_grouped0", [P, HALF_V, PACK], BF16)
@@ -199,98 +276,42 @@ def tile_picked_edgecv_relu_lo_kernel(
             z_codes, z_scales = quantize_z(1)
             out_grouped = sb("out_grouped1", [P, HALF_V, PACK], BF16)
             accs = []
-            for u in range(2):
-                acc = psum.tile([P, 2, HALF_V], F32, name=f"out_pair_acc{u}", tag=f"bank{4 * (1 - u)}")
-                for e in range(2):
-                    project(acc[:, e, :], 2 * u + e, z_codes, z_scales)
+            for u, number in enumerate((4, 0)):
+                acc = bank(f"out_pair_acc{u}", [P, 2, HALF_V], F32, number)
+                for n in range(2):
+                    project(acc[:, n, :], 2 * u + n, z_codes, z_scales)
                 accs.append(acc)
-            nc.scalar.copy(out_grouped[:, :, 0:2], accs[0][:].rearrange("p t v -> p v t"))
-            nc.vector.tensor_copy(out_grouped[:, :, 2:4], accs[1][:].rearrange("p t v -> p v t"))
+            nc.scalar.copy(out_grouped[:, :, LOW], accs[0][:].rearrange("p t v -> p v t"))
+            nc.vector.tensor_copy(out_grouped[:, :, HIGH], accs[1][:].rearrange("p t v -> p v t"))
             results = [sb(f"result_pair{u}", [P, 2, HALF_V], F32) for u in range(2)]
             nc.scalar.copy(results[0][:], accs[0][:])
             nc.vector.tensor_copy(results[1][:], accs[1][:])
-            nc.scalar.dma_start(out_rows[:, 0:2, second], results[0][:])
-            nc.sync.dma_start(out_rows[:, 2:4, second], results[1][:])
+            nc.scalar.dma_start(out_rows[:, LOW, second], results[0][:])
+            nc.sync.dma_start(out_rows[:, HIGH, second], results[1][:])
             quantize(out_codes[:, second], out_scales[:, second], out_grouped[:])
             nc.sync.dma_start(words_out[:, second], out_codes[:, second].bitcast(I32))
 
-        def gather(out, rows, lst, cols):
-            nc.vector.tensor_copy(out, rows[:].indirect(entries(lst, cols.start, cols.stop - cols.start)))
-
-        def gather_add(out, rows, lst, cols, other):
-            nc.vector.tensor_tensor(out, rows[:].indirect(entries(lst, cols.start, cols.stop - cols.start)), other, ADD)
-
-        turned_back = psum.tile([P, 2, 2, HALF_V], BF16, name="turned_back", tag="bank5")
-
-        def fetch(t, cols, fetched):
-            for d in range(4):
-                gather(fetched[d], e_rows[t], pos_t[d], cols)
-
-        def turned_step(t, fetched, banks):
-            centre = sb(f"centre{t}", [P, V], F32)
-            gather(centre[:], y_rows[t], cen_t, everyone)
-            edges = laid(f"edges{t}", [P, 2, 4, P], BF16, 2 * t)
-            for h, cols in enumerate((first, second)):
-                acc = psum.tile([P, 4, P], F32, name=f"edge_acc{t}_{h}", tag=f"bank{banks[h]}")
-                for d in range(4):
-                    nc.tensor.matmul(acc[:, d, :], fetched[d][:, cols], ident_f32[:], start=True, stop=False, is_transpose=True)
-                    nc.tensor.matmul(acc[:, d, :], centre[:, cols], ident_f32[:], start=False, stop=True, is_transpose=True)
-                nc.scalar.activation(edges[:, h, :, :], acc[:], RELU)
-            pairs = sb(f"edge_pairs{t}", [P, 2, 2, P], BF16)
-            nc.vector.tensor_tensor(pairs[:], edges[:, :, 0:2, :], edges[:, :, 2:4, :], MAX)
-            largest = sb(f"edge_largest{t}", [P, 2, P], BF16)
-            nc.vector.tensor_tensor(largest[:], pairs[:, :, 0, :], pairs[:, :, 1, :], MAX)
-            for h in range(2):
-                nc.tensor.transpose(turned_back[:, h, t, :], largest[:, h, :], ident_bf16[:])
-
-        def step(t, cols, kib):
-            n = cols.stop - cols.start
-            fetched = laid(f"fetched{t}", [P, 4, n], F32, kib)
-            fetch(t, cols, [fetched[:, d, :] for d in range(4)])
-            pairs = sb(f"pairs{t}", [P, 2, n], F32)
-            nc.vector.tensor_tensor(pairs[:], fetched[:, 0:2, :], fetched[:, 2:4, :], MAX)
-            largest = sb(f"largest{t}", [P, n], F32)
-            nc.vector.tensor_tensor(largest[:], pairs[:, 0, :], pairs[:, 1, :], MAX)
-            gather_add(sums[:, t, cols], y_rows[t], cen_t, cols, largest[:])
-
-        def last_step():
-            t = PACK - 1
-            part = laid("last", [P, 6, HALF_V], F32, 3)
-            g0, g1, gy, low, a2, w = [part[:, i, :] for i in range(6)]
-            gather(g0, e_rows[t], pos_t[0], second)
-            gather(g1, e_rows[t], pos_t[1], second)
-            gather(gy, y_rows[t], cen_t, second)
-            nc.vector.tensor_tensor(low, g0, g1, MAX)
-            gather_add(a2, e_rows[t], pos_t[2], second, gy)
-            nc.vector.tensor_tensor(w, low, gy, ADD)
-            gather_add(sums[:, PACK, second], e_rows[t], pos_t[3], second, gy)
-            nc.vector.tensor_tensor(sums[:, t, second], w, a2, MAX)
-            nc.vector.scalar_tensor_tensor(
-                z_grouped[1][:, :, 2:4],
-                sums[:, 2:4, second].rearrange("p j v -> p v j"),
-                0.0,
-                sums[:, 2:5:2, second].rearrange("p j v -> p v j"),
-                MAX,
-                MAX,
+        for part in range(DEAL_PARTS):
+            places = slice(part * P // DEAL_PARTS, (part + 1) * P // DEAL_PARTS)
+            nc.scalar.copy(
+                w3_grouped[:].rearrange("p (t m) j -> p m t j", t=PACK)[:, places],
+                w3_raw[:].rearrange("p j (m t) -> p m t j", t=PACK)[:, places],
             )
-
-        everyone = slice(0, V)
-        for part in range(4):
-            w3_deal(part)
         quantize(w3_codes[:], w3_scales[:], w3_grouped[:])
-        early = sb("early", [P, 6, V], F32)
-        held = laid("held", [P, 2, V], F32, 14)
-        fetched0 = [early[:, d, :] for d in range(4)]
-        fetched1 = [early[:, 4, :], early[:, 5, :], held[:, 0, :], held[:, 1, :]]
+
+        early = sb("early", [P, NEIGHBOURS + 2, V], F32)
+        held = laid("held", [P, 2, V], F32, Y_STAGE_AT)
+        fetched0 = [early[:, d, :] for d in range(NEIGHBOURS)]
+        fetched1 = [early[:, NEIGHBOURS, :], early[:, NEIGHBOURS + 1, :], held[:, 0, :], held[:, 1, :]]
         fetch(0, everyone, fetched0)
         fetch(1, everyone, fetched1)
         turned_step(0, fetched0, [3, 4])
         turned_step(1, fetched1, [6, 7])
-        y_rows.extend(hidden_rows("y23", *y23, [1, 2], [4, 6]))
+        y_rows.extend(hidden_rows("y23", y23, [1, 2], rows_at(Y_LATE_AT)))
         for h in range(2):
-            nc.scalar.copy(z_grouped[h][:, :, 0:2], turned_back[:, h, :, :].rearrange("p t v -> p v t"))
-        step(2, everyone, 8)
-        step(3, first, 0)
+            nc.scalar.copy(z_grouped[h][:, :, LOW], turned_back[:, h, :, :].rearrange("p t v -> p v t"))
+        vector_step(2, everyone, TILE2_FETCH_AT)
+        vector_step(3, first, TILE3_FETCH_AT)
         finish_first()
         last_step()
         finish_second()

from contextlib import ExitStack

import concourse.mybir as mybir
from concourse.masks import make_identity

K, T, S, V, H = 512, 1024, 512, 256, 512
FLOPS = 2 * (2 * K * H * S + H * H * V)

F32 = mybir.dt.float32
BF16 = mybir.dt.bfloat16
I32 = mybir.dt.int32
U32 = mybir.dt.uint32
U16 = mybir.dt.uint16
U8 = mybir.dt.uint8
FP8X4 = mybir.dt.float8_e4m3fn_x4
ADD = mybir.AluOpType.add
MAX = mybir.AluOpType.max
RELU = mybir.ActivationFunctionType.Relu

P = 128
PACK = 4
NEIGHBOURS = 4
LIST_ROWS = 16
BLOCK_ROWS = 8
LINE = 4
DEAL_PARTS = 4
HALF_S = S // 2
HALF_V = V // 2
LOW, HIGH = slice(0, 2), slice(2, 4)

W3_RAW_AT = 0
EDGES_AT = (0, 2)
Y_LATE_AT = (4, 6)
TILE3_FETCH_AT = 0
LAST_AT = 3
Y_EARLY_AT = (8, 12)
TILE2_FETCH_AT = 8
Y_STAGE_AT = 14


def tile_picked_edgecv_relu_lo_kernel(
    tc, xT, w1, w2, w3, offs, cen, pos1, pos2, pos3, pos4, out_0, out_1, out_2
):
    nc = tc.nc
    with ExitStack() as ctx:
        keep = ctx.enter_context(tc.tile_pool(name="keep", bufs=1))
        overlay = ctx.enter_context(tc.tile_pool(name="overlay", bufs=1))
        psum = ctx.enter_context(tc.psum_pool(name="psum", bufs=1))

        def sb(name, shape, dtype, tag=None):
            return keep.tile(shape, dtype, name=name, tag=tag or name, align_bytes=64)

        def laid(name, shape, dtype, kib):
            return overlay.tile(shape, dtype, name=name, offset=1024 * kib, align_bytes=64)

        def bank(name, shape, dtype, number):
            return psum.tile(shape, dtype, name=name, tag=f"bank{number}")

        def load_list(name, source):
            tile = keep.tile([P, source.shape[1]], U16, name=name)
            nc.sync.dma_start(tile[:], source)
            return tile

        def looked_up(rows, list_tile, cols):
            return rows[:].indirect(list_tile[:, cols.start // LIST_ROWS : cols.stop // LIST_ROWS])

        def gather(out, rows, list_tile, cols):
            nc.vector.tensor_copy(out, looked_up(rows, list_tile, cols))

        def gather_add(out, rows, list_tile, cols, other):
            nc.vector.tensor_tensor(out, looked_up(rows, list_tile, cols), other, ADD)

        def quantize(codes, scales, grouped):
            nc.vector.quantize_mx(out=codes.bitcast(FP8X4), scales=scales, in_=grouped.rearrange("p c j -> p (c j)"))

        def product(acc, w_codes, w_scales, moving_codes, moving_scales):
            nc.tensor.matmul_mx(
                out=acc,
                lhsT=w_codes.bitcast(FP8X4),
                lhsT_scale=w_scales,
                rhs=moving_codes.bitcast(FP8X4),
                rhs_scale=moving_scales,
                start=True,
                stop=True,
            )

        def weave_views(grouped, planes):
            return (
                grouped.rearrange("p (c i) j -> p c j i", i=LINE),
                planes.rearrange("p j (c i) -> p c j i", i=LINE),
            )

        ident_f32 = sb("ident_f32", [P, P], F32)
        make_identity(nc, ident_f32[:])
        ident_bf16 = sb("ident_bf16", [P, P], BF16)
        make_identity(nc, ident_bf16[:])

        offs_t = load_list("offs_t", offs)
        x_rows = xT.rearrange("(p j) c -> j p c", j=PACK)
        x_plane = [sb(f"x_plane{j}", [P, T], F32) for j in range(PACK)]
        for j in range(PACK):
            nc.sync.dma_start(x_plane[j][:], x_rows[j])
        w2_raw = sb("w2_raw", [P, PACK, H], F32)
        nc.sync.dma_start(w2_raw[:], w2.rearrange("(p j) c -> p j c", j=PACK))
        pos_t = [load_list(f"pos{d}_t", source) for d, source in enumerate((pos1, pos2, pos3, pos4))]
        w1_raw = sb("w1_raw", [P, PACK, H], F32)
        nc.sync.dma_start(w1_raw[:], w1.rearrange("(p j) c -> p j c", j=PACK))
        cen_t = load_list("cen_t", cen)
        w3_raw = laid("w3_raw", [P, PACK, H], F32, W3_RAW_AT)
        w3_rows = w3.rearrange("(b t q) c -> t b q c", t=PACK, q=BLOCK_ROWS)
        for t in range(PACK):
            nc.sync.dma_start(w3_raw[:, t, :], w3_rows[t])

        point_halves = (slice(0, HALF_S), slice(HALF_S, S))
        picked_low = sb("picked_low", [P, 2, S], F32)
        for j in range(2):
            nc.vector.tensor_copy(picked_low[:, j, :], x_plane[j][:].indirect(offs_t[:]))
        x_grouped = [sb(f"x_grouped{h}", [P, HALF_S, PACK], BF16) for h in range(2)]
        picked_high = [sb(f"picked_high{h}", [P, 2, HALF_S], F32) for h in range(2)]
        for h, points in enumerate(point_halves):
            nc.scalar.copy(*weave_views(x_grouped[h][:, :, LOW], picked_low[:, :, points]))
        for j in range(2):
            for h, points in enumerate(point_halves):
                gather(picked_high[h][:, j, :], x_plane[2 + j], offs_t, points)
        x_codes = sb("x_codes", [P, S], U32)
        x_scales = sb("x_scales", [P, S], U8)
        for h, copy in enumerate((nc.scalar.copy, nc.vector.tensor_copy)):
            copy(*weave_views(x_grouped[h][:, :, HIGH], picked_high[h][:]))
        for h, points in enumerate(point_halves):
            quantize(x_codes[:, points], x_scales[:, points], x_grouped[h][:])

        def stage_shape(tiles):
            return [P, len(tiles) * P, PACK]

        def hidden_weights(name, w_raw, tiles, copy, grouped):
            for n, t in enumerate(tiles):
                copy(
                    grouped[:, n * P : (n + 1) * P, :].rearrange("p (b u i) j -> p b u j i", u=2, i=LINE),
                    w_raw[:].rearrange("p j (b t u i) -> p t b u j i", t=PACK, u=2, i=LINE)[:, t],
                )
            codes = sb(f"{name}_codes", [P, len(tiles) * P], U32)
            scales = sb(f"{name}_scales", [P, len(tiles) * P], U8)
            quantize(codes[:], scales[:], grouped[:])
            return codes, scales

        def hidden_rows(name, weights, banks, make_rows):
            codes, scales = weights
            made = []
            for n, number in enumerate(banks):
                place = slice(n * P, (n + 1) * P)
                acc = bank(f"{name}_acc{n}", [P, S], F32, number)
                product(acc[:], codes[:, place], scales[:, place], x_codes[:], x_scales[:])
                rows = make_rows(f"{name}_rows{n}", n)
                nc.scalar.copy(rows[:], acc[:])
                made.append(rows)
            return made

        def own_rows(name, n):
            return sb(name, [P, S], F32)

        def rows_at(kibs):
            return lambda name, n: laid(name, [P, S], F32, kibs[n])

        e0_stage = sb("e0_grouped", stage_shape([0]), BF16, "w2_stage")
        e0_codes, e0_scales = hidden_weights("e0", w2_raw, [0], nc.scalar.copy, e0_stage)
        e_first = sb("e_first", [P, S], F32)
        for h, copy in enumerate((nc.scalar.copy, nc.vector.tensor_copy)):
            points = point_halves[h]
            acc = bank(f"e_first_acc{h}", [P, HALF_S], F32, h)
            product(acc[:], e0_codes[:], e0_scales[:], x_codes[:, points], x_scales[:, points])
            copy(e_first[:, points], acc[:])
        e12_stage = sb("e12_grouped", stage_shape([1, 2]), BF16, "w2_stage")
        e12 = hidden_weights("e12", w2_raw, [1, 2], nc.vector.tensor_copy, e12_stage)
        e3 = hidden_weights("e3", w2_raw, [3], nc.scalar.copy, sb("e3_grouped", stage_shape([3]), BF16))
        y01_stage = laid("y01_grouped", stage_shape([0, 1]), BF16, Y_STAGE_AT)
        y01 = hidden_weights("y01", w1_raw, [0, 1], nc.scalar.copy, y01_stage)
        e_rows = [e_first] + hidden_rows("e12", e12, [2, 3], own_rows) + hidden_rows("e3", e3, [4], own_rows)
        y_rows = hidden_rows("y01", y01, [5, 0], rows_at(Y_EARLY_AT))
        y23 = hidden_weights("y23", w1_raw, [2, 3], nc.scalar.copy, sb("y23_grouped", stage_shape([2, 3]), BF16))

        sums = sb("sums", [P, 3, V], F32)
        first, second, everyone = slice(0, HALF_V), slice(HALF_V, V), slice(0, V)

        w3_grouped = sb("w3_grouped", [P, H, PACK], BF16)
        w3_codes = sb("w3_codes", [P, H], U32)
        w3_scales = sb("w3_scales", [P, H], U8)
        out_codes = sb("out_codes", [P, V], U32)
        out_scales = sb("out_scales", [P, V], U8)
        out_rows = out_0.rearrange("(p t) v -> p t v", t=PACK)
        words_out = out_1.rearrange("z p c r -> p (z c r)").bitcast(I32)
        z_grouped = [sb(f"z_grouped{h}", [P, HALF_V, PACK], BF16) for h in range(2)]
        turned_back = bank("turned_back", [P, 2, 2, HALF_V], BF16, 5)

        def fetch(t, cols, fetched):
            for d in range(NEIGHBOURS):
                gather(fetched[d], e_rows[t], pos_t[d], cols)

        def turned_step(t, fetched, banks):
            centre = sb(f"centre{t}", [P, V], F32)
            gather(centre[:], y_rows[t], cen_t, everyone)
            edges = laid(f"edges{t}", [P, 2, NEIGHBOURS, P], BF16, EDGES_AT[t])
            for h, cols in enumerate((first, second)):
                acc = bank(f"edge_acc{t}_{h}", [P, NEIGHBOURS, P], F32, banks[h])
                for d in range(NEIGHBOURS):
                    nc.tensor.matmul(
                        acc[:, d, :], fetched[d][:, cols], ident_f32[:], start=True, stop=False, is_transpose=True
                    )
                    nc.tensor.matmul(
                        acc[:, d, :], centre[:, cols], ident_f32[:], start=False, stop=True, is_transpose=True
                    )
                nc.scalar.activation(edges[:, h, :, :], acc[:], RELU)
            pairs = sb(f"edge_pairs{t}", [P, 2, 2, P], BF16)
            nc.vector.tensor_tensor(pairs[:], edges[:, :, 0:2, :], edges[:, :, 2:4, :], MAX)
            largest = sb(f"edge_largest{t}", [P, 2, P], BF16)
            nc.vector.tensor_tensor(largest[:], pairs[:, :, 0, :], pairs[:, :, 1, :], MAX)
            for h in range(2):
                nc.tensor.transpose(turned_back[:, h, t, :], largest[:, h, :], ident_bf16[:])

        def vector_step(t, cols, kib):
            n = cols.stop - cols.start
            fetched = laid(f"fetched{t}", [P, NEIGHBOURS, n], F32, kib)
            fetch(t, cols, [fetched[:, d, :] for d in range(NEIGHBOURS)])
            pairs = sb(f"pairs{t}", [P, 2, n], F32)
            nc.vector.tensor_tensor(pairs[:], fetched[:, 0:2, :], fetched[:, 2:4, :], MAX)
            largest = sb(f"largest{t}", [P, n], F32)
            nc.vector.tensor_tensor(largest[:], pairs[:, 0, :], pairs[:, 1, :], MAX)
            gather_add(sums[:, t - 2, cols], y_rows[t], cen_t, cols, largest[:])

        def last_step():
            t = PACK - 1
            part = laid("last", [P, 6, HALF_V], F32, LAST_AT)
            near0, near1, centre, larger, edge2, edge01 = [part[:, n, :] for n in range(6)]
            gather(near0, e_rows[t], pos_t[0], second)
            gather(near1, e_rows[t], pos_t[1], second)
            gather(centre, y_rows[t], cen_t, second)
            nc.vector.tensor_tensor(larger, near0, near1, MAX)
            gather_add(edge2, e_rows[t], pos_t[2], second, centre)
            nc.vector.tensor_tensor(edge01, larger, centre, ADD)
            gather_add(sums[:, 2, second], e_rows[t], pos_t[3], second, centre)
            nc.vector.tensor_tensor(sums[:, 1, second], edge01, edge2, MAX)
            nc.vector.scalar_tensor_tensor(
                z_grouped[1][:, :, HIGH],
                sums[:, 0:2, second].rearrange("p j v -> p v j"),
                0.0,
                sums[:, 0:3:2, second].rearrange("p j v -> p v j"),
                MAX,
                MAX,
            )

        def quantize_z(h):
            z_codes = sb(f"z_codes{h}", [P, HALF_V], U32)
            z_scales = sb(f"z_scales{h}", [P, HALF_V], U8)
            quantize(z_codes[:], z_scales[:], z_grouped[h][:])
            return z_codes, z_scales

        def project(acc, t, z_codes, z_scales):
            place = slice(t * P, (t + 1) * P)
            product(acc, w3_codes[:, place], w3_scales[:, place], z_codes[:], z_scales[:])

        def finish_first():
            woven, planes = weave_views(z_grouped[0][:, :, HIGH], sums[:, 0:2, first])
            nc.scalar.activation(woven, planes, RELU)
            z_codes, z_scales = quantize_z(0)
            acc = bank("out_acc", [P, PACK, HALF_V], F32, 3)
            for t in range(PACK):
                project(acc[:, t, :], t, z_codes, z_scales)
            out_grouped = sb("out_grouped0", [P, HALF_V, PACK], BF16)
            result = sb("result0", [P, PACK, HALF_V], F32)
            nc.scalar.copy(out_grouped[:], acc[:].rearrange("p t v -> p v t"))
            nc.scalar.copy(result[:], acc[:])
            nc.sync.dma_start(out_rows[:, :, first], result[:])
            quantize(out_codes[:, first], out_scales[:, first], out_grouped[:])
            nc.sync.dma_start(words_out[:, first], out_codes[:, first].bitcast(I32))

        def finish_second():
            z_codes, z_scales = quantize_z(1)
            out_grouped = sb("out_grouped1", [P, HALF_V, PACK], BF16)
            accs = []
            for u, number in enumerate((4, 0)):
                acc = bank(f"out_pair_acc{u}", [P, 2, HALF_V], F32, number)
                for n in range(2):
                    project(acc[:, n, :], 2 * u + n, z_codes, z_scales)
                accs.append(acc)
            nc.scalar.copy(out_grouped[:, :, LOW], accs[0][:].rearrange("p t v -> p v t"))
            nc.vector.tensor_copy(out_grouped[:, :, HIGH], accs[1][:].rearrange("p t v -> p v t"))
            results = [sb(f"result_pair{u}", [P, 2, HALF_V], F32) for u in range(2)]
            nc.scalar.copy(results[0][:], accs[0][:])
            nc.vector.tensor_copy(results[1][:], accs[1][:])
            nc.scalar.dma_start(out_rows[:, LOW, second], results[0][:])
            nc.sync.dma_start(out_rows[:, HIGH, second], results[1][:])
            quantize(out_codes[:, second], out_scales[:, second], out_grouped[:])
            nc.sync.dma_start(words_out[:, second], out_codes[:, second].bitcast(I32))

        for part in range(DEAL_PARTS):
            places = slice(part * P // DEAL_PARTS, (part + 1) * P // DEAL_PARTS)
            nc.scalar.copy(
                w3_grouped[:].rearrange("p (t m) j -> p m t j", t=PACK)[:, places],
                w3_raw[:].rearrange("p j (m t) -> p m t j", t=PACK)[:, places],
            )
        quantize(w3_codes[:], w3_scales[:], w3_grouped[:])

        early = sb("early", [P, NEIGHBOURS + 2, V], F32)
        held = laid("held", [P, 2, V], F32, Y_STAGE_AT)
        fetched0 = [early[:, d, :] for d in range(NEIGHBOURS)]
        fetched1 = [early[:, NEIGHBOURS, :], early[:, NEIGHBOURS + 1, :], held[:, 0, :], held[:, 1, :]]
        fetch(0, everyone, fetched0)
        fetch(1, everyone, fetched1)
        turned_step(0, fetched0, [3, 4])
        turned_step(1, fetched1, [6, 7])
        y_rows.extend(hidden_rows("y23", y23, [1, 2], rows_at(Y_LATE_AT)))
        for h in range(2):
            nc.scalar.copy(z_grouped[h][:, :, LOW], turned_back[:, h, :, :].rearrange("p t v -> p v t"))
        vector_step(2, everyone, TILE2_FETCH_AT)
        vector_step(3, first, TILE3_FETCH_AT)
        finish_first()
        last_step()
        finish_second()

        scale_rows = out_2.rearrange("z q c -> (z q) c").bitcast(I32)
        for quad in range(4):
            queue = nc.sync if quad % 2 == 0 else nc.scalar
            queue.dma_start(scale_rows[4 * quad : 4 * quad + 4, :], out_scales[32 * quad : 32 * quad + 4, :].bitcast(I32))
